import numpy as np
import ml_dtypes


def mxq(x, axis, fmt="e4m3"):
    dtype, down = {"e4m3": (ml_dtypes.float8_e4m3fn, 7), "e5m2": (ml_dtypes.float8_e5m2, 14)}[fmt]
    v = np.moveaxis(np.asarray(x, np.float32).astype(ml_dtypes.bfloat16).astype(np.float64), axis, -1)
    blocks = v.reshape(v.shape[:-1] + (-1, 32))
    amax = np.abs(blocks).max(-1, keepdims=True)
    byte = np.maximum(np.where(amax > 0, np.frexp(amax)[1] - 1 + 127, 0) - down, 1)
    scale = np.exp2(byte - 127.0)
    codes = (blocks / scale).astype(np.float32).astype(dtype).astype(np.float64)
    return np.moveaxis((codes * scale).reshape(v.shape), -1, axis)


WIDE = False


def mx_kscale(k):
    if not WIDE:
        return np.ones(k)
    levels = np.array([10, -10, 5, -5, 0])
    if k % 512:
        return np.exp2(np.random.permutation(np.resize(levels, k // 32))).repeat(32)
    a = np.empty((k // 512, 16))
    for p in range(k // 512):
        a[p, :8] = np.random.permutation(np.resize(levels, 8))
        for g in range(8):
            far = levels[np.abs(levels - a[p, g]) >= 10]
            a[p, g + 8] = far[np.random.randint(len(far))]
    return np.exp2(a.ravel()).repeat(32)


BF16 = ml_dtypes.bfloat16


def bf(x):
    return np.asarray(x, np.float32).astype(BF16)


def f64(x):
    return np.asarray(x).astype(np.float64)

E4M3FN = np.array([(-1.0 if i & 128 else 1.0) * ((1.0 + (i & 7) / 8.0) * 2.0 ** (((i >> 3) & 15) - 7) if i & 120 else (i & 7) * 2.0 ** -9) for i in range(256)])


def e4m3fn_bytes(y):
    return np.clip(np.asarray(y, np.float64), -448.0, 448.0).astype(np.float32).astype(ml_dtypes.float8_e4m3fn).view(np.uint8)


def e4m3fn_values(b):
    return E4M3FN[b]


T, S, L, D, H, E, B = 512, 1536, 1024, 2048, 4, 512, 128


def setup_inputs():
    s, r, t = mx_kscale(L), mx_kscale(D), mx_kscale(E)
    wq = np.random.standard_normal((L, E * H)) / np.sqrt(L) / E ** 0.25 / s[:, None] * np.repeat(t, H)
    wk = np.random.standard_normal((E, D)) / np.sqrt(D) / E ** 0.25 / r
    wq_scale = (np.abs(wq).reshape(L // B, B, E * H // B, B).max(axis=(1, 3)) / 448).astype(np.float32)
    wk_scale = (np.abs(wk).reshape(E // B, B, D // B, B).max(axis=(1, 3)) / 448).astype(np.float32)
    return {"c": bf(np.random.standard_normal((T, L)) * s),
            "x": bf(np.random.standard_normal((S, D)) * r),
            "wq_bytes": e4m3fn_bytes(wq / np.repeat(np.repeat(f64(wq_scale), B, axis=0), B, axis=1)),
            "wq_scale": wq_scale,
            "wk_bytes": e4m3fn_bytes(wk / np.repeat(np.repeat(f64(wk_scale), B, axis=0), B, axis=1)),
            "wk_scale": wk_scale,
            "gk": bf((1 + 0.1 * np.random.standard_normal(E)) / t),
            "hw": bf(1 + 0.3 * np.random.standard_normal((T, H)))}


def reference(c, x, wq_bytes, wq_scale, wk_bytes, wk_scale, gk, hw):
    wq = e4m3fn_values(wq_bytes) * np.repeat(np.repeat(f64(wq_scale), B, axis=0), B, axis=1)
    wk = e4m3fn_values(wk_bytes) * np.repeat(np.repeat(f64(wk_scale), B, axis=0), B, axis=1)
    q = mxq(f64(c), 1, "e4m3") @ mxq(wq, 0, "e4m3")
    k = (mxq(f64(x), 1, "e4m3") @ mxq(wk, 1, "e4m3").T) * f64(gk)
    qh = q.reshape(T, E, H).swapaxes(1, 2).reshape(T * H, E)
    d = (mxq(qh, 1, "e4m3") @ mxq(k, 1, "e4m3").T).reshape(T, H, S)
    return np.sum(np.maximum(d, 0) * f64(hw)[:, :, None], axis=1)

from contextlib import ExitStack

import concourse.mybir as mybir
from concourse.masks import make_identity

T, S, L, D, H, E, B = 512, 1536, 1024, 2048, 4, 512, 128
FLOPS = 2 * (T * L * E * H + S * D * E + T * H * E * S)

F32 = mybir.dt.float32
BF16 = mybir.dt.bfloat16
U32 = mybir.dt.uint32
U8 = mybir.dt.uint8
FP8 = mybir.dt.float8_e4m3fn
FP8X4 = mybir.dt.float8_e4m3fn_x4
ALU = mybir.AluOpType
ACT = mybir.ActivationFunctionType

P = 128
PACK = 4
BANK = 512
Q_TILES = T // P
X_TILES = S // P
CHUNKS = S // BANK
Q_PASSES = L // (P * PACK)
K_PASSES = D // (P * PACK)
PARTS = 4
PART = E * H // PARTS
XB = 8
PB = 6
SF = [(1, 1), (3, 2)]


def tile_token_index_scores_d7_kernel(tc, c, x, wq_bytes, wq_scale, wk_bytes, wk_scale, gk, hw, out):
    nc = tc.nc
    with ExitStack() as ctx:
        keep = ctx.enter_context(tc.tile_pool(name="keep", bufs=1))
        work = ctx.enter_context(tc.tile_pool(name="work", bufs=2))
        psum = ctx.enter_context(tc.psum_pool(name="psum", bufs=8))
        ctx.enter_context(tc.manual_schedule())

        def mx_tiles(pool, name, words, tag=None, bufs=None):
            codes = pool.tile([P, words], U32, name=name + "_codes", tag=(tag or name) + "_codes", bufs=bufs, align_bytes=64)
            scales = pool.tile([P, words], U8, name=name + "_scales", tag=(tag or name) + "_scales", bufs=bufs, align_bytes=64)
            return codes, scales

        def quantize(mx, first, src):
            words = slice(first, first + src.shape[1] // PACK)
            nc.vector.quantize_mx(out=mx[0][:, words].bitcast(FP8X4), scales=mx[1][:, words], in_=src)

        def mx_pass(dst, lhs, lhs_cols, rhs, rhs_cols, start, stop):
            nc.tensor.matmul_mx(out=dst, lhsT=lhs[0][:, lhs_cols].bitcast(FP8X4), lhsT_scale=lhs[1][:, lhs_cols],
                                rhs=rhs[0][:, rhs_cols].bitcast(FP8X4), rhs_scale=rhs[1][:, rhs_cols], start=start, stop=stop)

        def cols(i, width=P):
            return slice(i * width, (i + 1) * width)

        def new_bank(name):
            bank = psum.tile([P, BANK], F32, name=name, tag="bank")
            return bank

        ident = keep.tile([P, P], F32, name="ident")
        make_identity(nc, ident[:])

        wk_sc = keep.tile([P, D // B], F32, name="wk_sc")
        wq_sc = keep.tile([P, Q_PASSES, E * H // B], F32, name="wq_sc")
        gk_raw = keep.tile([P, PACK], BF16, name="gk_raw")
        gk_rows = keep.tile([P, P, PACK], F32, name="gk_rows")
        hw_sb = keep.tile([P, Q_TILES, H], BF16, name="hw_sb")
        hw_f32 = keep.tile([P, Q_TILES], F32, name="hw_f32")
        wk_raw = [keep.tile([P, D], U8, name="wk_raw%d" % t) for t in range(PACK)]
        wq_raw = [keep.tile([P, PACK, PART], U8, name="wq_raw%d" % n) for n in range(Q_PASSES * PARTS)]
        c_raw = [keep.tile([P, L], BF16, name="c_raw%d" % i) for i in range(Q_TILES)]
        wk_mx = [mx_tiles(keep, "wk%d" % t, K_PASSES * P) for t in range(PACK)]
        wq_mx = [[mx_tiles(keep, "wq%d_%d" % (g, h), PACK * P) for h in range(H)] for g in range(Q_PASSES)]
        c_mx = [mx_tiles(keep, "c%d" % i, Q_PASSES * P) for i in range(Q_TILES)]
        key_mx = [mx_tiles(keep, "key%d" % n, BANK) for n in range(CHUNKS)]
        x_raw, rows, banks, packed, x_mx, q_mx, wq_wide, wq_packed, relus, sums = {}, {}, {}, {}, {}, {}, {}, {}, {}, {}

        wk_view = wk_bytes.rearrange("(m t) k -> t m k", t=PACK)
        wq_view = wq_bytes.rearrange("(g p j) (a n) -> g a p j n", p=P, j=PACK, a=PARTS)
        wq_sc_view = wq_scale.rearrange("(g q) b -> q g b", q=4)

        def load_x(i):
            x_raw[i] = work.tile([P, D], BF16, name="x_raw", tag="x_raw", bufs=XB)
            rows["x", i] = x_raw[i]
            nc.sync.dma_start(out=x_raw[i][:], in_=x[cols(i), :])

        def load_wk(t):
            nc.sync.dma_start(out=wk_raw[t][:], in_=wk_view[t])

        def load_wq(n):
            nc.sync.dma_start(out=wq_raw[n][:], in_=wq_view[n // PARTS, n % PARTS])

        def load_c(i):
            rows["c", i] = c_raw[i]
            nc.sync.dma_start(out=c_raw[i][:], in_=c[cols(i), :])

        def widen(engine, dst, src, scale):
            if engine == "vector":
                nc.vector.tensor_scalar(out=dst, in0=src.bitcast(FP8), scalar1=scale, scalar2=None, op0=ALU.mult)
            else:
                nc.scalar.activation(out=dst, in_=src.bitcast(FP8), func=ACT.Copy, scale=scale)

        def widen_wk(t, half):
            engine = "vector" if (widen_wk, t, half) in vector_order else "scalar"
            if ("wk", t) not in rows:
                rows["wk", t] = work.tile([P, D], BF16, name="wk_wide", tag="wk_wide", bufs=3)
            wide = rows["wk", t]
            for b in range(half * 8, half * 8 + 8):
                widen(engine, wide[:, cols(b)], wk_raw[t][:, cols(b)], wk_sc[:, b : b + 1])

        def turn(kind, i):
            words = rows[kind, i][:].bitcast(F32)
            for half in range(words.shape[1] // BANK):
                bank = new_bank("turn_" + kind)
                banks[kind, i, half] = bank
                for gu in range(4):
                    g, u = 2 * half + gu // 2, gu % 2
                    nc.tensor.transpose(bank[:, cols(gu)], words[:, 256 * g + u : 256 * (g + 1) : 2], ident[:])

        def spill(kind, i, half):
            engine = "vector" if (spill, kind, i, half) in vector_order else "scalar"
            if half == 0:
                packed[kind, i] = work.tile([P, rows[kind, i].shape[1]], BF16, name="packed_" + kind, tag="packed", bufs=PB, align_bytes=64)
            dst = packed[kind, i][:].bitcast(F32)[:, cols(half, BANK)].rearrange("p (g r u) -> p g r u", g=2, u=2)
            src = banks[kind, i, half][:].rearrange("p (g u r) -> p g r u", g=2, u=2)
            if engine == "vector":
                nc.vector.tensor_copy(out=dst, in_=src)
            else:
                nc.scalar.copy(out=dst, in_=src)

        def quant_wk(t):
            quantize(wk_mx[t], 0, packed["wk", t][:])

        def quant_c(i):
            quantize(c_mx[i], 0, packed["c", i][:])

        def quant_x(i):
            x_mx[i] = mx_tiles(work, "x", K_PASSES * P, bufs=6)
            quantize(x_mx[i], 0, packed["x", i][:])

        def key_matmul(i):
            bank = new_bank("key")
            banks["key", i] = bank
            for t in range(PACK):
                for g in range(K_PASSES):
                    mx_pass(bank[:, cols(t)], wk_mx[t], cols(g), x_mx[i], cols(g), g == 0, g == K_PASSES - 1)

        def key_spill(i):
            if i % 2 == 0:
                packed["key", i // 2] = work.tile([P, 2 * BANK], BF16, name="packed_key", tag="packed_key", bufs=2, align_bytes=64)
            dst = packed["key", i // 2][:, cols(i % 2, BANK)].rearrange("p (r t) -> p r t", t=PACK)
            nc.vector.tensor_tensor(out=dst, in0=banks["key", i][:].rearrange("p (t r) -> p r t", t=PACK), in1=gk_rows[:], op=ALU.mult)

        def quant_key(pair):
            quantize(key_mx[pair // 2], (pair % 2) * 2 * P, packed["key", pair][:])

        def widen_wq(n, j):
            engine = "vector" if (widen_wq, n, j) in vector_order else "scalar"
            if n not in wq_wide:
                wq_wide[n] = work.tile([P, PACK, PART], BF16, name="wq_wide", tag="wq_wide_" + engine, bufs=2)
            g, a = n // PARTS, n % PARTS
            for b in range(PART // B):
                blk = a * (PART // B) + b
                widen(engine, wq_wide[n][:, j, cols(b)], wq_raw[n][:, j, cols(b)], wq_sc[:, g, blk : blk + 1])

        def pack_wq(n):
            g, a = n // PARTS, n % PARTS
            if g not in wq_packed:
                wq_packed[g] = work.tile([P, E * H * PACK], BF16, name="wq_packed", tag="wq_packed", bufs=1, align_bytes=64)
            dst = wq_packed[g][:].rearrange("p (h t m j) -> p t m j h", h=H, t=PACK, j=PACK)[:, :, cols(a, P // PARTS)]
            nc.vector.tensor_copy(out=dst, in_=wq_wide[n][:].rearrange("p j (m t h) -> p t m j h", t=PACK, h=H))

        def quant_wq(g, h):
            quantize(wq_mx[g][h], 0, wq_packed[g][:, cols(h, PACK * BANK)])

        def q_matmul(i, h):
            bank = new_bank("q")
            banks["q", i, h] = bank
            for t in range(PACK):
                for g in range(Q_PASSES):
                    mx_pass(bank[:, cols(t)], wq_mx[g][h], cols(t), c_mx[i], cols(g), g == 0, g == Q_PASSES - 1)

        def q_spill(i, h):
            if h == 0:
                packed["q", i] = work.tile([P, H * BANK], BF16, name="packed_q", tag="packed", bufs=PB, align_bytes=64)
            dst = packed["q", i][:, cols(h, BANK)].rearrange("p (r t) -> p r t", t=PACK)
            nc.scalar.copy(out=dst, in_=banks["q", i, h][:].rearrange("p (t r) -> p r t", t=PACK))

        def quant_q(i, pair):
            if pair == 0:
                q_mx[i] = mx_tiles(work, "q", H * P, bufs=4)
            quantize(q_mx[i], pair * 2 * P, packed["q", i][:, cols(pair, 2 * BANK)])

        def dots(i, h, n):
            bank = new_bank("dots")
            banks["dots", i, h, n] = bank
            mx_pass(bank[:], q_mx[i], cols(h), key_mx[n], cols(0, BANK), True, True)

        def relu(i, h, n):
            relus[i, h, n] = work.tile([P, BANK], F32, name="relu", tag="relu", bufs=6)
            nc.scalar.activation(out=relus[i, h, n][:], in_=banks["dots", i, h, n][:], func=ACT.Relu)

        def add_head(i, h, n):
            weight = hw_sb[:, i, h : h + 1]
            if h == 0:
                sums[i, n] = work.tile([P, BANK], F32, name="total", tag="total", bufs=6)
            if h == 0 and (i, n) in scalar_first:
                nc.scalar.activation(out=sums[i, n][:], in_=relus[i, h, n][:], func=ACT.Copy, scale=hw_f32[:, i : i + 1])
            elif h == 0:
                nc.vector.tensor_scalar(out=sums[i, n][:], in0=banks["dots", i, h, n][:], scalar1=0.0, scalar2=weight, op0=ALU.max, op1=ALU.mult)
            else:
                nc.vector.scalar_tensor_tensor(out=sums[i, n][:], in0=relus[i, h, n][:], scalar=weight, in1=sums[i, n][:], op0=ALU.mult, op1=ALU.add)

        def store(i, n):
            nc.sync.dma_start(out=out[cols(i), cols(n, BANK)], in_=sums[i, n][:])

        def load_gk():
            nc.sync.dma_start(out=gk_raw[:], in_=gk.rearrange("(p t) -> p t", t=PACK))

        def load_hw():
            nc.sync.dma_start(out=hw_sb[:], in_=hw.rearrange("(i p) h -> p i h", p=P))

        def load_wq_scale(q):
            nc.sync.dma_start(out=wq_sc[cols(q, 32)], in_=wq_sc_view[q].partition_broadcast(32))

        def load_wk_scale(q):
            nc.sync.dma_start(out=wk_sc[cols(q, 32), :], in_=wk_scale[q].partition_broadcast(32))

        def widen_hw():
            nc.scalar.copy(out=hw_f32[:], in_=hw_sb[:, :, 0])

        def spread_gk():
            nc.scalar.activation(out=gk_rows[:], in_=gk_raw[:].unsqueeze(1).to_broadcast([P, P, PACK]), func=ACT.Copy)


        sync_order = [(load_wk, 0)] + [(load_wk_scale, q) for q in range(4)] + [(load_x, 0), (load_wk, 1), (load_wk, 2), (load_x, 1), (load_wk, 3), (load_x, 2), (load_gk,)]
        sync_order += [(load_wq_scale, q) for q in range(4)]
        sync_order += [(load_x, 3), (load_wq, 1), (load_wq, 0), (load_x, 4), (load_x, 5), (load_wq, 2), (load_wq, 3)]
        sync_order += [(load_c, i) for i in range(4)] + [(load_wq, 4), (load_x, 6), (load_x, 7), (load_wq, 5), (load_wq, 6), (load_wq, 7), (load_hw,)]
        sync_order += [(load_x, i) for i in range(8, 12)]
        units = [(0, 0), (0, 1), (1, 0), (1, 1), (0, 2), (1, 2)] + [(i, n) for i in (2, 3) for n in range(3)]
        scalar_first = SF
        sync_order += [(store, i, n) for i, n in units]

        def both(kind, *tiles):
            return [(spill, kind, i, half) for i in tiles for half in range(2)]

        def wide(n, js=range(4)):
            return [(widen_wq, n, j) for j in js]

        def each(fn, *items):
            return [(fn, i) for i in items]

        def turns(kind, *tiles):
            return [(turn, kind, i) for i in tiles]

        tensor_order = [(turn, "x", 0), (turn, "wk", 0), (turn, "wk", 1), (turn, "x", 1), (turn, "wk", 2), (turn, "wk", 3)] + turns("x", 2, 3)
        tensor_order += each(key_matmul, 0, 1) + turns("x", 4, 5) + each(key_matmul, 2, 3) + turns("c", 0, 1, 2, 3) + turns("x", 6, 7)
        tensor_order += each(key_matmul, 4, 5) + turns("x", 8, 9) + each(key_matmul, 6, 7) + turns("x", 10, 11) + each(key_matmul, 8, 9)
        tensor_order += [(q_matmul, 0, h) for h in range(4)]
        scalar_order = [(widen_wk, 0, 1)] + both("x", 0) + both("wk", 0, 1) + both("x", 1) + both("wk", 2, 3) + both("x", 2) + [(spread_gk,)] + both("x", 3)
        scalar_order += wide(0) + both("x", 4, 5) + wide(2) + [(spill, "c", i, 0) for i in range(4)] + both("x", 6, 7) + wide(4) + wide(5) + both("x", 8, 9) + wide(6) + wide(7)
        scalar_order += [(widen_hw,)] + both("x", 10, 11)
        scalar_order += [(q_spill, 0, h) for h in range(4)]
        vector_order = [(widen_wk, 0, 0)] + [(widen_wk, t, half) for t in (1, 2) for half in (0, 1)] + [(quant_x, 0), (quant_wk, 0), (widen_wk, 3, 0), (widen_wk, 3, 1), (quant_wk, 1), (quant_x, 1), (quant_wk, 2), (quant_wk, 3), (quant_x, 2)]
        vector_order += wide(1) + [(quant_x, 3), (key_spill, 0), (pack_wq, 1), (key_spill, 1), (pack_wq, 0), (quant_key, 0), (quant_x, 4), (quant_x, 5)] + wide(3)
        vector_order += [(key_spill, 2), (key_spill, 3), (pack_wq, 2), (quant_key, 1)] + each(quant_c, 0, 1, 2, 3) + [(pack_wq, 3), (quant_x, 6), (quant_x, 7)] + [(quant_wq, 0, h) for h in range(4)]
        vector_order += [(key_spill, 4), (key_spill, 5), (pack_wq, 4), (quant_key, 2), (pack_wq, 5), (key_spill, 6), (key_spill, 7), (quant_x, 8), (quant_x, 9), (pack_wq, 6), (quant_key, 3), (pack_wq, 7), (key_spill, 8)]
        vector_order += [(quant_wq, 1, h) for h in range(4)] + [(key_spill, 9), (quant_x, 10), (quant_q, 0, 0), (quant_x, 11), (quant_key, 4), (quant_q, 0, 1)]
        groups = [units[0:2], units[2:4], units[4:6], units[6:9], units[9:12]]
        ahead = [1, None, 2, 3, None]
        for gi, us in enumerate(groups):
            nxt = ahead[gi]
            for h in range(4):
                tensor_order += [(dots, i, h, n) for i, n in us]
                for i, n in us:
                    if h or (i, n) in scalar_first:
                        scalar_order += [(relu, i, h, n)]
                for i, n in us:
                    (scalar_order if h == 0 and (i, n) in scalar_first else vector_order).append((add_head, i, h, n))
                if gi == 0 and h in (1, 2):
                    tensor_order += [(key_matmul, 9 + h)]
                    vector_order += [(key_spill, 9 + h)]
                if gi == 1 and h == 0:
                    vector_order += [(quant_key, 5)]
                if nxt is not None:
                    tensor_order += [(q_matmul, nxt, h)]
                    scalar_order += [(q_spill, nxt, h)]
                    if h % 2:
                        vector_order += [(quant_q, nxt, h // 2)]

        def inputs_of(step):
            fn, args = step[0], step[1:]
            if fn == turn:
                return [(widen_wk, args[1], 0), (widen_wk, args[1], 1)] if args[0] == "wk" else [({"x": load_x, "c": load_c}[args[0]], args[1])]
            if fn == spill:
                return [(turn, args[0], args[1])]
            if fn == quant_wk:
                return [(spill, "wk", args[0], 1)]
            if fn == quant_x:
                return [(spill, "x", args[0], 1)]
            if fn == quant_c:
                return [(spill, "c", args[0], 0)]
            if fn == key_matmul:
                return [(quant_x, args[0])] + [(quant_wk, t) for t in range(PACK)]
            if fn == key_spill:
                return [(key_matmul, args[0]), (spread_gk,)]
            if fn == quant_key:
                return [(key_spill, 2 * args[0] + 1)]
            if fn == pack_wq:
                return [(widen_wq, args[0], j) for j in range(PACK)]
            if fn == quant_wq:
                return [(pack_wq, args[0] * PARTS + a) for a in range(PARTS)]
            if fn == q_matmul:
                return [(quant_c, args[0])] + [(quant_wq, g, args[1]) for g in range(Q_PASSES)]
            if fn == q_spill:
                return [(q_matmul,) + args]
            if fn == quant_q:
                return [(q_spill, args[0], 2 * args[1] + 1)]
            if fn == dots:
                return [(quant_q, args[0], args[1] // 2), (quant_key, 2 * args[2] + 1)]
            if fn == relu:
                return [(dots,) + args]
            if fn == add_head:
                if args[1]:
                    return [(relu,) + args, (add_head, args[0], args[1] - 1, args[2])]
                return [(relu,) + args, (widen_hw,)] if (args[0], args[2]) in scalar_first else [(dots,) + args]
            if fn == store:
                return [(add_head, args[0], H - 1, args[1])]
            if fn == widen_wq:
                return [(load_wq, args[0])]
            if fn == widen_wk:
                return [(load_wk, args[0])]
            if fn == spread_gk:
                return [(load_gk,)]
            if fn == widen_hw:
                return [(load_hw,)]
            return []

        done = set()
        queues = [sync_order, tensor_order, scalar_order, vector_order]
        heads = [0] * len(queues)
        while any(heads[e] < len(queues[e]) for e in range(len(queues))):
            moved = False
            for e, queue in enumerate(queues):
                while heads[e] < len(queue) and all(s in done for s in inputs_of(queue[heads[e]])):
                    step = queue[heads[e]]
                    step[0](*step[1:])
                    done.add(step)
                    heads[e] += 1
                    moved = True
            assert moved
